import numpy as np
import ml_dtypes


def mxq(x, axis, fmt="e4m3"):
    dtype, down = {"e4m3": (ml_dtypes.float8_e4m3fn, 7), "e5m2": (ml_dtypes.float8_e5m2, 14)}[fmt]
    v = np.moveaxis(np.asarray(x, np.float32).astype(ml_dtypes.bfloat16).astype(np.float64), axis, -1)
    blocks = v.reshape(v.shape[:-1] + (-1, 32))
    amax = np.abs(blocks).max(-1, keepdims=True)
    byte = np.maximum(np.where(amax > 0, np.frexp(amax)[1] - 1 + 127, 0) - down, 1)
    scale = np.exp2(byte - 127.0)
    codes = (blocks / scale).astype(np.float32).astype(dtype).astype(np.float64)
    return np.moveaxis((codes * scale).reshape(v.shape), -1, axis)


WIDE = False


def mx_kscale(k):
    if not WIDE:
        return np.ones(k)
    levels = np.array([10, -10, 5, -5, 0])
    if k % 512:
        return np.exp2(np.random.permutation(np.resize(levels, k // 32))).repeat(32)
    a = np.empty((k // 512, 16))
    for p in range(k // 512):
        a[p, :8] = np.random.permutation(np.resize(levels, 8))
        for g in range(8):
            far = levels[np.abs(levels - a[p, g]) >= 10]
            a[p, g + 8] = far[np.random.randint(len(far))]
    return np.exp2(a.ravel()).repeat(32)


def f64(x):
    return np.asarray(x).astype(np.float64)


def striped(idx):
    return np.tile(idx.reshape(-1, 16).T, (8, 1)).astype(np.uint16)


def unstriped(offs):
    return offs[:16].T.reshape(-1).astype(np.int64)


def pack_weight(w):
    k, n = w.shape
    w = f64(np.asarray(w, np.float32).astype(ml_dtypes.bfloat16)).reshape(k // 32, 32, n)
    amax = np.abs(w).max(1)
    byte = np.clip(np.where(amax > 0, np.frexp(amax)[1] - 1 + 127 - 7, 1), 1, 254)
    scaled = (w * np.exp2(127.0 - byte)[:, None, :]).reshape(k, n).astype(np.float32)
    words = np.ascontiguousarray(scaled.reshape(k // 512, 128, 4, n).transpose(0, 1, 3, 2)).astype(ml_dtypes.float8_e4m3fn).view(np.uint8)
    return words, np.ascontiguousarray(byte.astype(np.uint8).reshape(k // 512, 16, n))


def unpack_weight(words, scales):
    g, p, n, _ = words.shape
    vals = np.ascontiguousarray(words).view(ml_dtypes.float8_e4m3fn).astype(np.float64) * np.repeat(np.exp2(scales.astype(np.float64) - 127.0), 8, axis=1)[..., None]
    return vals.transpose(0, 1, 3, 2).reshape(g * 512, n)


K, T, D, S, V, N = 512, 2048, 4, 2048, 512, 512
P = 2 ** 7


def setup_inputs():
    n = np.random.standard_normal
    s = mx_kscale(K)[:, None]
    words, scales = pack_weight(n((K, N)) / np.sqrt(K) / s)
    return {
        "xT": (n((K, T)) * s / np.sqrt(D)).astype(ml_dtypes.bfloat16).astype(np.float32),
        "w_words": words,
        "w_scales": scales,
        "b": (0.3 * n((N, 1))).astype(np.float32),
        "gate": np.tile(np.random.uniform(0.5, 1.5, (D, 1, V)), (1, P, 1)).astype(ml_dtypes.bfloat16).astype(np.float32),
        "offs": striped(np.concatenate([np.random.permutation(T)[:V] for _ in range(D)])),
    }


def reference(xT, w_words, w_scales, b, gate, offs):
    w = unpack_weight(w_words, w_scales)
    idx = unstriped(offs)
    x = sum(f64(gate)[d, :1] * f64(xT)[:, idx[d * V:(d + 1) * V]] for d in range(D))
    return (w.T @ mxq(x, 0, "e4m3")) + f64(b)

@@ -1,0 +1,183 @@
+from contextlib import ExitStack
+
+import concourse.mybir as mybir
+from concourse.masks import make_identity
+
+K, T, D, V, N = 512, 2048, 4, 512, 512
+FLOPS = 2 * K * V * N
+
+F32 = mybir.dt.float32
+BF16 = mybir.dt.bfloat16
+U32 = mybir.dt.uint32
+I32 = mybir.dt.int32
+U16 = mybir.dt.uint16
+U8 = mybir.dt.uint8
+FP8X4 = mybir.dt.float8_e4m3fn_x4
+MULT = mybir.AluOpType.mult
+ADD = mybir.AluOpType.add
+COPY = mybir.ActivationFunctionType.Copy
+
+P = 128
+PACK = 4
+BLOCKS = V // P
+HALF = V // 2
+ROW_STEP = 13
+PAIR_CHUNKS = [896, 640, 512]
+
+
+def gate_column(d, block):
+    return min(i for i in range(P) if (ROW_STEP * i) // (P * BLOCKS) == d and (ROW_STEP * i) % BLOCKS == block)
+
+
+def tile_picked_bag_lin_bias_sub_l_kernel(tc, xT, w_words, w_scales, b, gate, offs, out):
+    nc = tc.nc
+    with ExitStack() as ctx:
+        keep = ctx.enter_context(tc.tile_pool(name="keep", bufs=1))
+        psum = ctx.enter_context(tc.psum_pool(name="psum", bufs=1))
+
+        offsets = keep.tile([P, D * V // 16], U16, name="offsets")
+        gate_rows = keep.tile([P, P], F32, name="gate_rows")
+        gate_cols = keep.tile([P, P], F32, name="gate_cols")
+        gate_wide = [keep.tile([P, V], F32, name=f"gate_wide{d}") for d in range(D)]
+        ident = keep.tile([P, P], F32, name="ident")
+        warm = keep.tile([P, 8], F32, name="warm")
+        rows2 = keep.tile([P, T], F32, name="rows2")
+        rows3 = keep.tile([P, T], F32, name="rows3")
+        rows0 = keep.tile([P, 2 * T], BF16, name="rows0")
+        rows01 = keep.tile([P, 2 * T], BF16, name="rows01")
+        w_codes = keep.tile([P, N], U32, name="w_codes", align_bytes=64)
+        w_plane = keep.tile([P, N], U8, name="w_plane", align_bytes=64)
+        bias = keep.tile([P, N // P], F32, name="bias")
+        final = [psum.tile([P, PACK, P], F32, name=f"final{j}") for j in range(BLOCKS)]
+        turn = [psum.tile([P, PACK, P], F32, name=f"turn{j}") for j in range(4)]
+
+        x_rows = xT.rearrange("(p t) c -> p t c", t=PACK)
+        x_halves = xT.bitcast(BF16).rearrange("(p t) c -> p t c", t=PACK)
+
+        def entries(d, first, count):
+            return offsets[:, (d * V + first) // 16 : (d * V + first + count) // 16]
+
+        nc.sync.dma_start(gate_rows[:], gate.rearrange("d p (j v) -> (d p j) v", v=P)[0 : ROW_STEP * P : ROW_STEP, :])
+        nc.sync.dma_start(offsets[:], offs)
+        nc.sync.dma_start(rows2[:], x_rows[:, 2, :])
+        chunks = []
+        first = 0
+        for width in PAIR_CHUNKS:
+            chunks.append((first, first + width))
+            first += width
+        for c0, c1 in chunks:
+            nc.sync.dma_start(rows01[:, 2 * c0 : 2 * c1], x_halves[:, 1, 2 * c0 : 2 * c1])
+            nc.sync.dma_start(rows0[:, 2 * c0 : 2 * c1], x_halves[:, 0, 2 * c0 : 2 * c1])
+        nc.sync.dma_start(rows3[:], x_rows[:, 3, :])
+        nc.sync.dma_start(w_codes[:].bitcast(I32), w_words[0].rearrange("p n t -> p (n t)").bitcast(I32))
+        nc.vector.memset(w_plane[:].bitcast(I32), 0)
+        for q in range(4):
+            nc.sync.dma_start(
+                w_plane[32 * q : 32 * q + 4, :].bitcast(I32), w_scales[0, 4 * q : 4 * q + 4, :].bitcast(I32)
+            )
+        with nc.allow_non_contiguous_dma(reason="one bias value a partition"):
+            nc.sync.dma_start(bias[:], b.rearrange("(j p) o -> p (j o)", p=P))
+
+        nc.vector.memset(warm[:], 0.0)
+        nc.scalar.activation(warm[:, 0:1], warm[:, 4:5], COPY)
+        make_identity(nc, ident[:])
+
+        nc.tensor.transpose(turn[3][:, 0, :], gate_rows[:], ident[:])
+        nc.vector.tensor_copy(gate_cols[:], turn[3][:, 0, :])
+        for d in range(D):
+            for j in range(BLOCKS):
+                i = gate_column(d, j)
+                nc.tensor.transpose(final[d][:, j, :], gate_cols[:, i : i + 1].to_broadcast([P, P]), ident[:])
+            src = final[d][:].rearrange("p j v -> p (j v)")
+            if d == 0:
+                nc.vector.tensor_copy(gate_wide[d][:], src)
+            else:
+                nc.scalar.activation(gate_wide[d][:], src, COPY)
+
+        prod2 = keep.tile([P, D, V], F32, name="prod2")
+        for d in range(D):
+            nc.vector.tensor_tensor(prod2[:, d, :], rows2[:].indirect(entries(d, 0, V)), gate_wide[d][:], MULT)
+            for j in range(BLOCKS):
+                nc.tensor.matmul(
+                    turn[j][:, 0, :], lhsT=prod2[:, d, j * P : (j + 1) * P], rhs=ident[:],
+                    start=(d == 0), stop=(d == D - 1), is_transpose=True,
+                )
+
+        nc.scalar.activation(warm[:, 1:2], gate_wide[D - 1][:, 0:1], COPY, scale=rows01[:, 0:2].bitcast(F32))
+        for c0, c1 in chunks:
+            c0 = max(c0 - 8, 0)
+            nc.scalar.activation(rows01[:, 2 * c0 : 2 * c1 : 2], rows0[:, 2 * c0 + 1 : 2 * c1 : 2], COPY)
+        pairs = rows01[:].bitcast(U32)
+
+        sum2 = keep.tile([P, BLOCKS, P], F32, name="sum2")
+        for j in range(BLOCKS):
+            nc.scalar.activation(sum2[:, j, :], turn[j][:, 0, :], COPY)
+            nc.tensor.transpose(final[j][:, 2, :], sum2[:, j, :], ident[:])
+
+        picked = keep.tile([P, 2, D, HALF], U32, name="picked")
+        weighted = keep.tile([P, BLOCKS, D, 2, P], F32, name="weighted")
+        prod3 = picked[:].rearrange("p h d v -> p (h d v)").bitcast(F32).rearrange("p (j d v) -> p j d v", j=BLOCKS, d=D)
+        sum3 = keep.tile([P, BLOCKS, P], F32, name="sum3")
+        grouped = keep.tile([P, BLOCKS, P, PACK], BF16, name="grouped", align_bytes=64)
+        x_codes = keep.tile([P, BLOCKS, P], U32, name="x_codes", align_bytes=64)
+        x_plane = [keep.tile([P, P], U8, name=f"x_plane{j}", align_bytes=64) for j in range(BLOCKS)]
+        result = keep.tile([P, BLOCKS, N // P, P], F32, name="result")
+        out_view = out.rearrange("(m p) v -> p m v", p=P)
+
+        for h in range(2):
+            for d in range(D):
+                bank = turn[(2 * h + d) % 4]
+                nc.vector.tensor_copy(picked[:, h, d, :], pairs.indirect(entries(d, h * HALF, HALF)))
+                for s in range(2):
+                    nc.tensor.transpose(bank[:, s, :], picked[:, h, d, s * P : (s + 1) * P].bitcast(F32), ident[:])
+                for s in range(2):
+                    j = 2 * h + s
+                    i = gate_column(d, j)
+                    nc.scalar.activation(
+                        weighted[:, j, d, :, :],
+                        bank[:, s, :].bitcast(BF16).rearrange("v (p e) -> v e p", e=2),
+                        COPY,
+                        scale=gate_cols[:, i : i + 1],
+                    )
+            for s in range(2):
+                j = 2 * h + s
+                for e in range(2):
+                    for d in range(D):
+                        nc.tensor.matmul(
+                            final[j][:, e, :], lhsT=weighted[:, j, d, e, :], rhs=ident[:],
+                            start=(d == 0), stop=(d == D - 1), is_transpose=True,
+                        )
+            for s in range(2):
+                j = 2 * h + s
+                bank = turn[j]
+                for d in range(D):
+                    nc.vector.tensor_tensor(
+                        prod3[:, j, d, :], rows3[:].indirect(entries(d, j * P, P)),
+                        gate_wide[d][:, j * P : (j + 1) * P], MULT,
+                    )
+                    nc.tensor.matmul(
+                        bank[:, 2, :], lhsT=prod3[:, j, d, :], rhs=ident[:],
+                        start=(d == 0), stop=(d == D - 1), is_transpose=True,
+                    )
+                nc.scalar.activation(sum3[:, j, :], bank[:, 2, :], COPY)
+                nc.tensor.transpose(final[j][:, 3, :], sum3[:, j, :], ident[:])
+                nc.scalar.activation(grouped[:, j, :, :], final[j][:].rearrange("p t v -> p v t"), COPY)
+            for s in range(2):
+                j = 2 * h + s
+                nc.vector.quantize_mx(
+                    out=x_codes[:, j, :].bitcast(FP8X4), scales=x_plane[j][:],
+                    in_=grouped[:, j, :, :].rearrange("p v t -> p (v t)"),
+                )
+                for m in range(N // P):
+                    nc.tensor.matmul_mx(
+                        out=final[j][:, m, :],
+                        lhsT=w_codes[:, m * P : (m + 1) * P].bitcast(FP8X4),
+                        lhsT_scale=w_plane[:, m * P : (m + 1) * P],
+                        rhs=x_codes[:, j, :].bitcast(FP8X4),
+                        rhs_scale=x_plane[j][:],
+                        start=True, stop=True,
+                    )
+                nc.vector.tensor_tensor(
+                    result[:, j, :, :], final[j][:], bias[:].unsqueeze(2).to_broadcast([P, N // P, P]), ADD
+                )
+                nc.sync.dma_start(out_view[:, :, j * P : (j + 1) * P], result[:, j, :, :])

@@ -16,13 +16,14 @@ FP8X4 = mybir.dt.float8_e4m3fn_x4
 MULT = mybir.AluOpType.mult
 ADD = mybir.AluOpType.add
 COPY = mybir.ActivationFunctionType.Copy
+IDENTITY = mybir.ActivationFunctionType.Identity
 
 P = 128
 PACK = 4
 BLOCKS = V // P
 HALF = V // 2
 ROW_STEP = 13
-PAIR_CHUNKS = [896, 640, 512]
+PAIR_CHUNKS = [896, 704, 448]
 
 
 def gate_column(d, block):
@@ -41,6 +42,7 @@ def tile_picked_bag_lin_bias_sub_l_kernel(tc, xT, w_words, w_scales, b, gate, of
         gate_wide = [keep.tile([P, V], F32, name=f"gate_wide{d}") for d in range(D)]
         ident = keep.tile([P, P], F32, name="ident")
         warm = keep.tile([P, 8], F32, name="warm")
+        marks = keep.tile([P, 8], F32, name="marks")
         rows2 = keep.tile([P, T], F32, name="rows2")
         rows3 = keep.tile([P, T], F32, name="rows3")
         rows0 = keep.tile([P, 2 * T], BF16, name="rows0")
@@ -92,41 +94,43 @@ def tile_picked_bag_lin_bias_sub_l_kernel(tc, xT, w_words, w_scales, b, gate, of
             if d == 0:
                 nc.vector.tensor_copy(gate_wide[d][:], src)
             else:
-                nc.scalar.activation(gate_wide[d][:], src, COPY)
+                nc.scalar.activation(gate_wide[d][:], src, COPY, accum_out=marks[:, d : d + 1])
 
         prod2 = keep.tile([P, D, V], F32, name="prod2")
         for d in range(D):
             nc.vector.tensor_tensor(prod2[:, d, :], rows2[:].indirect(entries(d, 0, V)), gate_wide[d][:], MULT)
             for j in range(BLOCKS):
                 nc.tensor.matmul(
-                    turn[j][:, 0, :], lhsT=prod2[:, d, j * P : (j + 1) * P], rhs=ident[:],
+                    turn[(j + 1) % 4][:, 2, :], lhsT=prod2[:, d, j * P : (j + 1) * P], rhs=ident[:],
                     start=(d == 0), stop=(d == D - 1), is_transpose=True,
                 )
 
-        nc.scalar.activation(warm[:, 1:2], gate_wide[D - 1][:, 0:1], COPY, scale=rows01[:, 0:2].bitcast(F32))
-        for c0, c1 in chunks:
-            c0 = max(c0 - 8, 0)
-            nc.scalar.activation(rows01[:, 2 * c0 : 2 * c1 : 2], rows0[:, 2 * c0 + 1 : 2 * c1 : 2], COPY)
+        for c, (c0, c1) in enumerate(chunks):
+            c0 -= 8 if c1 == T else 0
+            low, source = rows01[:, 2 * c0 : 2 * c1 : 2], rows0[:, 2 * c0 + 1 : 2 * c1 : 2]
+            if c1 < T:
+                nc.scalar.activation(low, source, COPY, accum_out=marks[:, 2 + c : 3 + c])
+            else:
+                nc.vector.tensor_copy(low, source)
         pairs = rows01[:].bitcast(U32)
-
-        sum2 = keep.tile([P, BLOCKS, P], F32, name="sum2")
-        for j in range(BLOCKS):
-            nc.scalar.activation(sum2[:, j, :], turn[j][:, 0, :], COPY)
-            nc.tensor.transpose(final[j][:, 2, :], sum2[:, j, :], ident[:])
 
         picked = keep.tile([P, 2, D, HALF], U32, name="picked")
         weighted = keep.tile([P, BLOCKS, D, 2, P], F32, name="weighted")
         prod3 = picked[:].rearrange("p h d v -> p (h d v)").bitcast(F32).rearrange("p (j d v) -> p j d v", j=BLOCKS, d=D)
-        sum3 = keep.tile([P, BLOCKS, P], F32, name="sum3")
+        sums = keep.tile([P, BLOCKS, 2, P], F32, name="sums")
         grouped = keep.tile([P, BLOCKS, P, PACK], BF16, name="grouped", align_bytes=64)
         x_codes = keep.tile([P, BLOCKS, P], U32, name="x_codes", align_bytes=64)
         x_plane = [keep.tile([P, P], U8, name=f"x_plane{j}", align_bytes=64) for j in range(BLOCKS)]
         result = keep.tile([P, BLOCKS, N // P, P], F32, name="result")
         out_view = out.rearrange("(m p) v -> p m v", p=P)
+        last = BLOCKS - 1
+
+        nc.scalar.activation(sums[:, last, 0, :], turn[0][:, 2, :], COPY, accum_out=marks[:, 2:3])
+        nc.tensor.transpose(final[last][:, 2, :], sums[:, last, 0, :], ident[:])
 
         for h in range(2):
             for d in range(D):
-                bank = turn[(2 * h + d) % 4]
+                bank = turn[d]
                 nc.vector.tensor_copy(picked[:, h, d, :], pairs.indirect(entries(d, h * HALF, HALF)))
                 for s in range(2):
                     nc.tensor.transpose(bank[:, s, :], picked[:, h, d, s * P : (s + 1) * P].bitcast(F32), ident[:])
@@ -139,45 +143,76 @@ def tile_picked_bag_lin_bias_sub_l_kernel(tc, xT, w_words, w_scales, b, gate, of
                         COPY,
                         scale=gate_cols[:, i : i + 1],
                     )
-            for s in range(2):
-                j = 2 * h + s
-                for e in range(2):
-                    for d in range(D):
+                    for e in range(2):
                         nc.tensor.matmul(
                             final[j][:, e, :], lhsT=weighted[:, j, d, e, :], rhs=ident[:],
-                            start=(d == 0), stop=(d == D - 1), is_transpose=True,
+                            start=(d == 0 and e == 0), stop=(d == D - 1 and e == 1), is_transpose=True,
                         )
-            for s in range(2):
-                j = 2 * h + s
-                bank = turn[j]
-                for d in range(D):
-                    nc.vector.tensor_tensor(
-                        prod3[:, j, d, :], rows3[:].indirect(entries(d, j * P, P)),
-                        gate_wide[d][:, j * P : (j + 1) * P], MULT,
-                    )
-                    nc.tensor.matmul(
-                        bank[:, 2, :], lhsT=prod3[:, j, d, :], rhs=ident[:],
-                        start=(d == 0), stop=(d == D - 1), is_transpose=True,
-                    )
-                nc.scalar.activation(sum3[:, j, :], bank[:, 2, :], COPY)
-                nc.tensor.transpose(final[j][:, 3, :], sum3[:, j, :], ident[:])
-                nc.scalar.activation(grouped[:, j, :, :], final[j][:].rearrange("p t v -> p v t"), COPY)
-            for s in range(2):
-                j = 2 * h + s
-                nc.vector.quantize_mx(
-                    out=x_codes[:, j, :].bitcast(FP8X4), scales=x_plane[j][:],
-                    in_=grouped[:, j, :, :].rearrange("p v t -> p (v t)"),
+
+        def gather3(j, d, dest):
+            nc.vector.tensor_tensor(dest, rows3[:].indirect(entries(d, j * P, P)), gate_wide[d][:, j * P : (j + 1) * P], MULT)
+
+        def spent(j):
+            return grouped[:, j, :, :].rearrange("p v t -> p (v t)").bitcast(F32)[:, 0:P]
+
+        def quantize(j):
+            nc.vector.quantize_mx(
+                out=x_codes[:, j, :].bitcast(FP8X4), scales=x_plane[j][:],
+                in_=grouped[:, j, :, :].rearrange("p v t -> p (v t)"),
+            )
+
+        def product(j, on_vector):
+            spare = final[j] if on_vector == 0 else turn[j - 1]
+            for m in range(N // P):
+                nc.tensor.matmul_mx(
+                    out=(final[j] if m < on_vector else spare)[:, m, :],
+                    lhsT=w_codes[:, m * P : (m + 1) * P].bitcast(FP8X4),
+                    lhsT_scale=w_plane[:, m * P : (m + 1) * P],
+                    rhs=x_codes[:, j, :].bitcast(FP8X4),
+                    rhs_scale=x_plane[j][:],
+                    start=True, stop=True,
                 )
-                for m in range(N // P):
-                    nc.tensor.matmul_mx(
-                        out=final[j][:, m, :],
-                        lhsT=w_codes[:, m * P : (m + 1) * P].bitcast(FP8X4),
-                        lhsT_scale=w_plane[:, m * P : (m + 1) * P],
-                        rhs=x_codes[:, j, :].bitcast(FP8X4),
-                        rhs_scale=x_plane[j][:],
-                        start=True, stop=True,
-                    )
+            if on_vector:
                 nc.vector.tensor_tensor(
-                    result[:, j, :, :], final[j][:], bias[:].unsqueeze(2).to_broadcast([P, N // P, P]), ADD
+                    result[:, j, 0:on_vector, :], final[j][:, 0:on_vector, :],
+                    bias[:, 0:on_vector].unsqueeze(2).to_broadcast([P, on_vector, P]), ADD,
                 )
-                nc.sync.dma_start(out_view[:, :, j * P : (j + 1) * P], result[:, j, :, :])
+            for m in range(on_vector, N // P):
+                nc.scalar.activation(result[:, j, m, :], spare[:, m, :], IDENTITY, bias=bias[:, m : m + 1])
+            nc.sync.dma_start(out_view[:, :, j * P : (j + 1) * P], result[:, j, :, :])
+
+        for j in range(last):
+            bank = turn[j + 1]
+            for d in range(D):
+                gather3(j, d, prod3[:, j, d, :])
+                nc.tensor.matmul(
+                    bank[:, 3, :], lhsT=prod3[:, j, d, :], rhs=ident[:],
+                    start=(d == 0), stop=(d == D - 1), is_transpose=True,
+                )
+            if j == 2:
+                nc.scalar.activation(sums[:, j, :, :], bank[:, 2:4, :], COPY, accum_out=marks[:, 4:5])
+                nc.scalar.activation(grouped[:, last, :, 0:3], final[last][:, 0:3, :].rearrange("p t v -> p v t"), COPY)
+            else:
+                nc.scalar.activation(sums[:, j, :, :], bank[:, 2:4, :], COPY)
+            for e in range(2):
+                nc.tensor.transpose(final[j][:, 2 + e, :], sums[:, j, e, :], ident[:])
+            if j == 0:
+                nc.scalar.activation(grouped[:, j, :, :], final[j][:].rearrange("p t v -> p v t"), COPY, accum_out=marks[:, 4:5])
+            else:
+                nc.scalar.activation(grouped[:, j, :, :], final[j][:].rearrange("p t v -> p v t"), COPY)
+
+        quantize(0)
+        quantize(1)
+        gather3(last, 0, prod3[:, last, 0, :])
+        gather3(last, 1, prod3[:, last, 1, :])
+        gather3(last, 2, spent(0))
+        nc.vector.tensor_tensor(prod3[:, last, 2, :], prod3[:, last, 0, :], prod3[:, last, 1, :], ADD)
+        gather3(last, 3, prod3[:, last, 3, :])
+        nc.vector.tensor_tensor(spent(1), prod3[:, last, 2, :], spent(0), ADD)
+        nc.vector.tensor_tensor(grouped[:, last, :, 3], spent(1), prod3[:, last, 3, :], ADD)
+        quantize(last)
+        quantize(2)
+        product(0, 0)
+        product(1, 4)
+        product(last, 2)
+        product(2, 2)

@@ -23,7 +23,7 @@ PACK = 4
 BLOCKS = V // P
 HALF = V // 2
 ROW_STEP = 13
-PAIR_CHUNKS = [896, 704, 448]
+PAIR_CHUNKS = [1024, 384, 640]
 
 
 def gate_column(d, block):
@@ -68,7 +68,8 @@ def tile_picked_bag_lin_bias_sub_l_kernel(tc, xT, w_words, w_scales, b, gate, of
             chunks.append((first, first + width))
             first += width
         for c0, c1 in chunks:
-            nc.sync.dma_start(rows01[:, 2 * c0 : 2 * c1], x_halves[:, 1, 2 * c0 : 2 * c1])
+            if c0 % (T // 2) == 0:
+                nc.sync.dma_start(rows01[:, 2 * c0 : 2 * c0 + T], x_halves[:, 1, 2 * c0 : 2 * c0 + T])
             nc.sync.dma_start(rows0[:, 2 * c0 : 2 * c1], x_halves[:, 0, 2 * c0 : 2 * c1])
         nc.sync.dma_start(rows3[:], x_rows[:, 3, :])
         nc.sync.dma_start(w_codes[:].bitcast(I32), w_words[0].rearrange("p n t -> p (n t)").bitcast(I32))
@@ -89,16 +90,22 @@ def tile_picked_bag_lin_bias_sub_l_kernel(tc, xT, w_words, w_scales, b, gate, of
         for d in range(D):
             for j in range(BLOCKS):
                 i = gate_column(d, j)
-                nc.tensor.transpose(final[d][:, j, :], gate_cols[:, i : i + 1].to_broadcast([P, P]), ident[:])
+                bank = turn[0][:, j - 2, :] if d == 0 and j >= 2 else final[d][:, j, :]
+                nc.tensor.transpose(bank, gate_cols[:, i : i + 1].to_broadcast([P, P]), ident[:])
             src = final[d][:].rearrange("p j v -> p (j v)")
             if d == 0:
-                nc.vector.tensor_copy(gate_wide[d][:], src)
+                nc.vector.tensor_copy(gate_wide[d][:, 0:HALF], src[:, 0:HALF])
+                nc.scalar.activation(gate_wide[d][:, HALF:V], turn[0][:, 0:2, :].rearrange("p j v -> p (j v)"), COPY)
             else:
                 nc.scalar.activation(gate_wide[d][:], src, COPY, accum_out=marks[:, d : d + 1])
 
         prod2 = keep.tile([P, D, V], F32, name="prod2")
         for d in range(D):
-            nc.vector.tensor_tensor(prod2[:, d, :], rows2[:].indirect(entries(d, 0, V)), gate_wide[d][:], MULT)
+            for first, count in ((0, HALF), (HALF, HALF)) if d == 0 else ((0, V),):
+                cols = slice(first, first + count)
+                nc.vector.tensor_tensor(
+                    prod2[:, d, cols], rows2[:].indirect(entries(d, first, count)), gate_wide[d][:, cols], MULT
+                )
             for j in range(BLOCKS):
                 nc.tensor.matmul(
                     turn[(j + 1) % 4][:, 2, :], lhsT=prod2[:, d, j * P : (j + 1) * P], rhs=ident[:],
@@ -121,7 +128,7 @@ def tile_picked_bag_lin_bias_sub_l_kernel(tc, xT, w_words, w_scales, b, gate, of
         grouped = keep.tile([P, BLOCKS, P, PACK], BF16, name="grouped", align_bytes=64)
         x_codes = keep.tile([P, BLOCKS, P], U32, name="x_codes", align_bytes=64)
         x_plane = [keep.tile([P, P], U8, name=f"x_plane{j}", align_bytes=64) for j in range(BLOCKS)]
-        result = keep.tile([P, BLOCKS, N // P, P], F32, name="result")
+        result = keep.tile([P, 2, N // P, HALF], F32, name="result")
         out_view = out.rearrange("(m p) v -> p m v", p=P)
         last = BLOCKS - 1
 
@@ -149,8 +156,26 @@ def tile_picked_bag_lin_bias_sub_l_kernel(tc, xT, w_words, w_scales, b, gate, of
                             start=(d == 0 and e == 0), stop=(d == D - 1 and e == 1), is_transpose=True,
                         )
 
-        def gather3(j, d, dest):
-            nc.vector.tensor_tensor(dest, rows3[:].indirect(entries(d, j * P, P)), gate_wide[d][:, j * P : (j + 1) * P], MULT)
+        def gather3(d, first, count, dest):
+            nc.vector.tensor_tensor(
+                dest, rows3[:].indirect(entries(d, first, count)), gate_wide[d][:, first : first + count], MULT
+            )
+
+        def add_turned(j, d, source):
+            nc.tensor.matmul(
+                turn[j + 1][:, 3, :], lhsT=source, rhs=ident[:],
+                start=(d == 0), stop=(d == D - 1), is_transpose=True,
+            )
+
+        def turn_back(j, mark):
+            nc.scalar.activation(sums[:, j, :, :], turn[j + 1][:, 2:4, :], COPY, accum_out=mark)
+            for e in range(2):
+                nc.tensor.transpose(final[j][:, 2 + e, :], sums[:, j, e, :], ident[:])
+
+        def interleave(j, count, mark):
+            nc.scalar.activation(
+                grouped[:, j, :, 0:count], final[j][:, 0:count, :].rearrange("p t v -> p v t"), COPY, accum_out=mark
+            )
 
         def spent(j):
             return grouped[:, j, :, :].rearrange("p v t -> p (v t)").bitcast(F32)[:, 0:P]
@@ -162,10 +187,11 @@ def tile_picked_bag_lin_bias_sub_l_kernel(tc, xT, w_words, w_scales, b, gate, of
             )
 
         def product(j, on_vector):
-            spare = final[j] if on_vector == 0 else turn[j - 1]
+            other = final[j] if on_vector == 0 else turn[j - 1]
+            dest = result[:, j // 2, :, (j % 2) * P : (j % 2 + 1) * P]
             for m in range(N // P):
                 nc.tensor.matmul_mx(
-                    out=(final[j] if m < on_vector else spare)[:, m, :],
+                    out=(final[j] if m < on_vector else other)[:, m, :],
                     lhsT=w_codes[:, m * P : (m + 1) * P].bitcast(FP8X4),
                     lhsT_scale=w_plane[:, m * P : (m + 1) * P],
                     rhs=x_codes[:, j, :].bitcast(FP8X4),
@@ -174,45 +200,48 @@ def tile_picked_bag_lin_bias_sub_l_kernel(tc, xT, w_words, w_scales, b, gate, of
                 )
             if on_vector:
                 nc.vector.tensor_tensor(
-                    result[:, j, 0:on_vector, :], final[j][:, 0:on_vector, :],
+                    dest[:, 0:on_vector, :], final[j][:, 0:on_vector, :],
                     bias[:, 0:on_vector].unsqueeze(2).to_broadcast([P, on_vector, P]), ADD,
                 )
             for m in range(on_vector, N // P):
-                nc.scalar.activation(result[:, j, m, :], spare[:, m, :], IDENTITY, bias=bias[:, m : m + 1])
-            nc.sync.dma_start(out_view[:, :, j * P : (j + 1) * P], result[:, j, :, :])
+                nc.scalar.activation(dest[:, m, :], other[:, m, :], IDENTITY, bias=bias[:, m : m + 1])
 
-        for j in range(last):
-            bank = turn[j + 1]
+        def store(h):
+            nc.sync.dma_start(out_view[:, :, h * HALF : (h + 1) * HALF], result[:, h, :, :])
+
+        def sum3(j):
             for d in range(D):
-                gather3(j, d, prod3[:, j, d, :])
-                nc.tensor.matmul(
-                    bank[:, 3, :], lhsT=prod3[:, j, d, :], rhs=ident[:],
-                    start=(d == 0), stop=(d == D - 1), is_transpose=True,
-                )
-            if j == 2:
-                nc.scalar.activation(sums[:, j, :, :], bank[:, 2:4, :], COPY, accum_out=marks[:, 4:5])
-                nc.scalar.activation(grouped[:, last, :, 0:3], final[last][:, 0:3, :].rearrange("p t v -> p v t"), COPY)
-            else:
-                nc.scalar.activation(sums[:, j, :, :], bank[:, 2:4, :], COPY)
-            for e in range(2):
-                nc.tensor.transpose(final[j][:, 2 + e, :], sums[:, j, e, :], ident[:])
-            if j == 0:
-                nc.scalar.activation(grouped[:, j, :, :], final[j][:].rearrange("p t v -> p v t"), COPY, accum_out=marks[:, 4:5])
-            else:
-                nc.scalar.activation(grouped[:, j, :, :], final[j][:].rearrange("p t v -> p v t"), COPY)
+                gather3(d, j * P, P, prod3[:, j, d, :])
+                add_turned(j, d, prod3[:, j, d, :])
+
+        sum3(0)
+        turn_back(0, None)
+        interleave(last, PACK - 1, marks[:, 5:6])
+        interleave(0, PACK, marks[:, 4:5])
+        sum3(1)
+        turn_back(1, marks[:, 5:6])
+        sum3(2)
+        turn_back(2, marks[:, 4:5])
+        interleave(1, PACK, None)
+        interleave(2, PACK, None)
 
         quantize(0)
-        quantize(1)
-        gather3(last, 0, prod3[:, last, 0, :])
-        gather3(last, 1, prod3[:, last, 1, :])
-        gather3(last, 2, spent(0))
+        gather3(0, last * P, P, prod3[:, last, 0, :])
+        gather3(1, last * P, P, prod3[:, last, 1, :])
+        gather3(2, last * P, P, spent(0))
         nc.vector.tensor_tensor(prod3[:, last, 2, :], prod3[:, last, 0, :], prod3[:, last, 1, :], ADD)
-        gather3(last, 3, prod3[:, last, 3, :])
-        nc.vector.tensor_tensor(spent(1), prod3[:, last, 2, :], spent(0), ADD)
-        nc.vector.tensor_tensor(grouped[:, last, :, 3], spent(1), prod3[:, last, 3, :], ADD)
-        quantize(last)
+        gather3(3, last * P, P, prod3[:, last, 3, :])
+        nc.vector.tensor_tensor(prod3[:, last, 0, :], prod3[:, last, 2, :], spent(0), ADD)
+        quantize(1)
+        nc.vector.scalar_tensor_tensor(
+            grouped[:, last, :, 3], prod3[:, last, 0, :], 1.0, prod3[:, last, 3, :], MULT, ADD,
+            accum_out=spent(1)[:, 0:1],
+        )
         quantize(2)
+        quantize(last)
         product(0, 0)
-        product(1, 4)
-        product(last, 2)
+        product(1, 0)
+        store(0)
         product(2, 2)
+        product(last, 2)
+        store(1)

@@ -121,9 +121,9 @@ def tile_picked_bag_lin_bias_sub_l_kernel(tc, xT, w_words, w_scales, b, gate, of
                 nc.vector.tensor_copy(low, source)
         pairs = rows01[:].bitcast(U32)
 
-        picked = keep.tile([P, 2, D, HALF], U32, name="picked")
+        picked = keep.tile([P, D, V], U32, name="picked")
         weighted = keep.tile([P, BLOCKS, D, 2, P], F32, name="weighted")
-        prod3 = picked[:].rearrange("p h d v -> p (h d v)").bitcast(F32).rearrange("p (j d v) -> p j d v", j=BLOCKS, d=D)
+        prod3 = picked[:].rearrange("p d v -> p (d v)").bitcast(F32).rearrange("p (j d v) -> p j d v", j=BLOCKS, d=D)
         sums = keep.tile([P, BLOCKS, 2, P], F32, name="sums")
         grouped = keep.tile([P, BLOCKS, P, PACK], BF16, name="grouped", align_bytes=64)
         x_codes = keep.tile([P, BLOCKS, P], U32, name="x_codes", align_bytes=64)
@@ -135,12 +135,14 @@ def tile_picked_bag_lin_bias_sub_l_kernel(tc, xT, w_words, w_scales, b, gate, of
         nc.scalar.activation(sums[:, last, 0, :], turn[0][:, 2, :], COPY, accum_out=marks[:, 2:3])
         nc.tensor.transpose(final[last][:, 2, :], sums[:, last, 0, :], ident[:])
 
-        for h in range(2):
-            for d in range(D):
-                bank = turn[d]
-                nc.vector.tensor_copy(picked[:, h, d, :], pairs.indirect(entries(d, h * HALF, HALF)))
+        for d in range(D):
+            for first, count in ((0, HALF), (HALF, HALF)) if d == 0 else ((0, V),):
+                nc.vector.tensor_copy(picked[:, d, first : first + count], pairs.indirect(entries(d, first, count)))
+            for h in range(2):
+                bank = turn[(2 * d + h) % 4]
                 for s in range(2):
-                    nc.tensor.transpose(bank[:, s, :], picked[:, h, d, s * P : (s + 1) * P].bitcast(F32), ident[:])
+                    j = 2 * h + s
+                    nc.tensor.transpose(bank[:, s, :], picked[:, d, j * P : (j + 1) * P].bitcast(F32), ident[:])
                 for s in range(2):
                     j = 2 * h + s
                     i = gate_column(d, j)

from contextlib import ExitStack

import concourse.mybir as mybir
from concourse.masks import make_identity

K, T, D, V, N = 512, 2048, 4, 512, 512
FLOPS = 2 * K * V * N

F32 = mybir.dt.float32
BF16 = mybir.dt.bfloat16
U32 = mybir.dt.uint32
I32 = mybir.dt.int32
U16 = mybir.dt.uint16
U8 = mybir.dt.uint8
FP8X4 = mybir.dt.float8_e4m3fn_x4
MULT = mybir.AluOpType.mult
ADD = mybir.AluOpType.add
COPY = mybir.ActivationFunctionType.Copy
IDENTITY = mybir.ActivationFunctionType.Identity

P = 128
PACK = 4
BLOCKS = V // P
HALF = V // 2
ROW_STEP = 13
PAIR_CHUNKS = [1024, 384, 640]


def gate_column(d, block):
    return min(i for i in range(P) if (ROW_STEP * i) // (P * BLOCKS) == d and (ROW_STEP * i) % BLOCKS == block)


def tile_picked_bag_lin_bias_sub_l_kernel(tc, xT, w_words, w_scales, b, gate, offs, out):
    nc = tc.nc
    with ExitStack() as ctx:
        keep = ctx.enter_context(tc.tile_pool(name="keep", bufs=1))
        psum = ctx.enter_context(tc.psum_pool(name="psum", bufs=1))

        offsets = keep.tile([P, D * V // 16], U16, name="offsets")
        gate_rows = keep.tile([P, P], F32, name="gate_rows")
        gate_cols = keep.tile([P, P], F32, name="gate_cols")
        gate_wide = [keep.tile([P, V], F32, name=f"gate_wide{d}") for d in range(D)]
        ident = keep.tile([P, P], F32, name="ident")
        warm = keep.tile([P, 8], F32, name="warm")
        marks = keep.tile([P, 8], F32, name="marks")
        rows2 = keep.tile([P, T], F32, name="rows2")
        rows3 = keep.tile([P, T], F32, name="rows3")
        rows0 = keep.tile([P, 2 * T], BF16, name="rows0")
        rows01 = keep.tile([P, 2 * T], BF16, name="rows01")
        w_codes = keep.tile([P, N], U32, name="w_codes", align_bytes=64)
        w_plane = keep.tile([P, N], U8, name="w_plane", align_bytes=64)
        bias = keep.tile([P, N // P], F32, name="bias")
        final = [psum.tile([P, PACK, P], F32, name=f"final{j}") for j in range(BLOCKS)]
        turn = [psum.tile([P, PACK, P], F32, name=f"turn{j}") for j in range(4)]

        x_rows = xT.rearrange("(p t) c -> p t c", t=PACK)
        x_halves = xT.bitcast(BF16).rearrange("(p t) c -> p t c", t=PACK)

        def entries(d, first, count):
            return offsets[:, (d * V + first) // 16 : (d * V + first + count) // 16]

        nc.sync.dma_start(gate_rows[:], gate.rearrange("d p (j v) -> (d p j) v", v=P)[0 : ROW_STEP * P : ROW_STEP, :])
        nc.sync.dma_start(offsets[:], offs)
        nc.sync.dma_start(rows2[:], x_rows[:, 2, :])
        chunks = []
        first = 0
        for width in PAIR_CHUNKS:
            chunks.append((first, first + width))
            first += width
        for c0, c1 in chunks:
            if c0 % (T // 2) == 0:
                nc.sync.dma_start(rows01[:, 2 * c0 : 2 * c0 + T], x_halves[:, 1, 2 * c0 : 2 * c0 + T])
            nc.sync.dma_start(rows0[:, 2 * c0 : 2 * c1], x_halves[:, 0, 2 * c0 : 2 * c1])
        nc.sync.dma_start(rows3[:], x_rows[:, 3, :])
        nc.sync.dma_start(w_codes[:].bitcast(I32), w_words[0].rearrange("p n t -> p (n t)").bitcast(I32))
        nc.vector.memset(w_plane[:].bitcast(I32), 0)
        for q in range(4):
            nc.sync.dma_start(
                w_plane[32 * q : 32 * q + 4, :].bitcast(I32), w_scales[0, 4 * q : 4 * q + 4, :].bitcast(I32)
            )
        with nc.allow_non_contiguous_dma(reason="one bias value a partition"):
            nc.sync.dma_start(bias[:], b.rearrange("(j p) o -> p (j o)", p=P))

        nc.vector.memset(warm[:], 0.0)
        nc.scalar.activation(warm[:, 0:1], warm[:, 4:5], COPY)
        make_identity(nc, ident[:])

        nc.tensor.transpose(turn[3][:, 0, :], gate_rows[:], ident[:])
        nc.vector.tensor_copy(gate_cols[:], turn[3][:, 0, :])
        for d in range(D):
            for j in range(BLOCKS):
                i = gate_column(d, j)
                bank = turn[0][:, j - 2, :] if d == 0 and j >= 2 else final[d][:, j, :]
                nc.tensor.transpose(bank, gate_cols[:, i : i + 1].to_broadcast([P, P]), ident[:])
            src = final[d][:].rearrange("p j v -> p (j v)")
            if d == 0:
                nc.vector.tensor_copy(gate_wide[d][:, 0:HALF], src[:, 0:HALF])
                nc.scalar.activation(gate_wide[d][:, HALF:V], turn[0][:, 0:2, :].rearrange("p j v -> p (j v)"), COPY)
            else:
                nc.scalar.activation(gate_wide[d][:], src, COPY, accum_out=marks[:, d : d + 1])

        prod2 = keep.tile([P, D, V], F32, name="prod2")
        for d in range(D):
            for first, count in ((0, HALF), (HALF, HALF)) if d == 0 else ((0, V),):
                cols = slice(first, first + count)
                nc.vector.tensor_tensor(
                    prod2[:, d, cols], rows2[:].indirect(entries(d, first, count)), gate_wide[d][:, cols], MULT
                )
            for j in range(BLOCKS):
                nc.tensor.matmul(
                    turn[(j + 1) % 4][:, 2, :], lhsT=prod2[:, d, j * P : (j + 1) * P], rhs=ident[:],
                    start=(d == 0), stop=(d == D - 1), is_transpose=True,
                )

        for c, (c0, c1) in enumerate(chunks):
            c0 -= 8 if c1 == T else 0
            low, source = rows01[:, 2 * c0 : 2 * c1 : 2], rows0[:, 2 * c0 + 1 : 2 * c1 : 2]
            if c1 < T:
                nc.scalar.activation(low, source, COPY, accum_out=marks[:, 2 + c : 3 + c])
            else:
                nc.vector.tensor_copy(low, source)
        pairs = rows01[:].bitcast(U32)

        picked = keep.tile([P, D, V], U32, name="picked")
        weighted = keep.tile([P, BLOCKS, D, 2, P], F32, name="weighted")
        prod3 = picked[:].rearrange("p d v -> p (d v)").bitcast(F32).rearrange("p (j d v) -> p j d v", j=BLOCKS, d=D)
        sums = keep.tile([P, BLOCKS, 2, P], F32, name="sums")
        grouped = keep.tile([P, BLOCKS, P, PACK], BF16, name="grouped", align_bytes=64)
        x_codes = keep.tile([P, BLOCKS, P], U32, name="x_codes", align_bytes=64)
        x_plane = [keep.tile([P, P], U8, name=f"x_plane{j}", align_bytes=64) for j in range(BLOCKS)]
        result = keep.tile([P, 2, N // P, HALF], F32, name="result")
        out_view = out.rearrange("(m p) v -> p m v", p=P)
        last = BLOCKS - 1

        nc.scalar.activation(sums[:, last, 0, :], turn[0][:, 2, :], COPY, accum_out=marks[:, 2:3])
        nc.tensor.transpose(final[last][:, 2, :], sums[:, last, 0, :], ident[:])

        for d in range(D):
            for first, count in ((0, HALF), (HALF, HALF)) if d == 0 else ((0, V),):
                nc.vector.tensor_copy(picked[:, d, first : first + count], pairs.indirect(entries(d, first, count)))
            for h in range(2):
                bank = turn[(2 * d + h) % 4]
                for s in range(2):
                    j = 2 * h + s
                    nc.tensor.transpose(bank[:, s, :], picked[:, d, j * P : (j + 1) * P].bitcast(F32), ident[:])
                for s in range(2):
                    j = 2 * h + s
                    i = gate_column(d, j)
                    nc.scalar.activation(
                        weighted[:, j, d, :, :],
                        bank[:, s, :].bitcast(BF16).rearrange("v (p e) -> v e p", e=2),
                        COPY,
                        scale=gate_cols[:, i : i + 1],
                    )
                    for e in range(2):
                        nc.tensor.matmul(
                            final[j][:, e, :], lhsT=weighted[:, j, d, e, :], rhs=ident[:],
                            start=(d == 0 and e == 0), stop=(d == D - 1 and e == 1), is_transpose=True,
                        )

        def gather3(d, first, count, dest):
            nc.vector.tensor_tensor(
                dest, rows3[:].indirect(entries(d, first, count)), gate_wide[d][:, first : first + count], MULT
            )

        def add_turned(j, d, source):
            nc.tensor.matmul(
                turn[j + 1][:, 3, :], lhsT=source, rhs=ident[:],
                start=(d == 0), stop=(d == D - 1), is_transpose=True,
            )

        def turn_back(j, mark):
            nc.scalar.activation(sums[:, j, :, :], turn[j + 1][:, 2:4, :], COPY, accum_out=mark)
            for e in range(2):
                nc.tensor.transpose(final[j][:, 2 + e, :], sums[:, j, e, :], ident[:])

        def interleave(j, count, mark):
            nc.scalar.activation(
                grouped[:, j, :, 0:count], final[j][:, 0:count, :].rearrange("p t v -> p v t"), COPY, accum_out=mark
            )

        def spent(j):
            return grouped[:, j, :, :].rearrange("p v t -> p (v t)").bitcast(F32)[:, 0:P]

        def quantize(j):
            nc.vector.quantize_mx(
                out=x_codes[:, j, :].bitcast(FP8X4), scales=x_plane[j][:],
                in_=grouped[:, j, :, :].rearrange("p v t -> p (v t)"),
            )

        def product(j, on_vector):
            other = final[j] if on_vector == 0 else turn[j - 1]
            dest = result[:, j // 2, :, (j % 2) * P : (j % 2 + 1) * P]
            for m in range(N // P):
                nc.tensor.matmul_mx(
                    out=(final[j] if m < on_vector else other)[:, m, :],
                    lhsT=w_codes[:, m * P : (m + 1) * P].bitcast(FP8X4),
                    lhsT_scale=w_plane[:, m * P : (m + 1) * P],
                    rhs=x_codes[:, j, :].bitcast(FP8X4),
                    rhs_scale=x_plane[j][:],
                    start=True, stop=True,
                )
            if on_vector:
                nc.vector.tensor_tensor(
                    dest[:, 0:on_vector, :], final[j][:, 0:on_vector, :],
                    bias[:, 0:on_vector].unsqueeze(2).to_broadcast([P, on_vector, P]), ADD,
                )
            for m in range(on_vector, N // P):
                nc.scalar.activation(dest[:, m, :], other[:, m, :], IDENTITY, bias=bias[:, m : m + 1])

        def store(h):
            nc.sync.dma_start(out_view[:, :, h * HALF : (h + 1) * HALF], result[:, h, :, :])

        def sum3(j):
            for d in range(D):
                gather3(d, j * P, P, prod3[:, j, d, :])
                add_turned(j, d, prod3[:, j, d, :])

        sum3(0)
        turn_back(0, None)
        interleave(last, PACK - 1, marks[:, 5:6])
        interleave(0, PACK, marks[:, 4:5])
        sum3(1)
        turn_back(1, marks[:, 5:6])
        sum3(2)
        turn_back(2, marks[:, 4:5])
        interleave(1, PACK, None)
        interleave(2, PACK, None)

        quantize(0)
        gather3(0, last * P, P, prod3[:, last, 0, :])
        gather3(1, last * P, P, prod3[:, last, 1, :])
        gather3(2, last * P, P, spent(0))
        nc.vector.tensor_tensor(prod3[:, last, 2, :], prod3[:, last, 0, :], prod3[:, last, 1, :], ADD)
        gather3(3, last * P, P, prod3[:, last, 3, :])
        nc.vector.tensor_tensor(prod3[:, last, 0, :], prod3[:, last, 2, :], spent(0), ADD)
        quantize(1)
        nc.vector.scalar_tensor_tensor(
            grouped[:, last, :, 3], prod3[:, last, 0, :], 1.0, prod3[:, last, 3, :], MULT, ADD,
            accum_out=spent(1)[:, 0:1],
        )
        quantize(2)
        quantize(last)
        product(0, 0)
        product(1, 0)
        store(0)
        product(2, 2)
        product(last, 2)
        store(1)
